import numpy as np
import ml_dtypes


def mxq(x, axis, fmt="e4m3"):
    dtype, down = {"e4m3": (ml_dtypes.float8_e4m3fn, 7), "e5m2": (ml_dtypes.float8_e5m2, 14)}[fmt]
    v = np.moveaxis(np.asarray(x, np.float32).astype(ml_dtypes.bfloat16).astype(np.float64), axis, -1)
    blocks = v.reshape(v.shape[:-1] + (-1, 32))
    amax = np.abs(blocks).max(-1, keepdims=True)
    byte = np.maximum(np.where(amax > 0, np.frexp(amax)[1] - 1 + 127, 0) - down, 1)
    scale = np.exp2(byte - 127.0)
    codes = (blocks / scale).astype(np.float32).astype(dtype).astype(np.float64)
    return np.moveaxis((codes * scale).reshape(v.shape), -1, axis)


WIDE = False


def mx_kscale(k):
    if not WIDE:
        return np.ones(k)
    levels = np.array([10, -10, 5, -5, 0])
    if k % 512:
        return np.exp2(np.random.permutation(np.resize(levels, k // 32))).repeat(32)
    a = np.empty((k // 512, 16))
    for p in range(k // 512):
        a[p, :8] = np.random.permutation(np.resize(levels, 8))
        for g in range(8):
            far = levels[np.abs(levels - a[p, g]) >= 10]
            a[p, g + 8] = far[np.random.randint(len(far))]
    return np.exp2(a.ravel()).repeat(32)


def f64(x):
    return np.asarray(x).astype(np.float64)


def striped(idx):
    return np.tile(idx.reshape(-1, 16).T, (8, 1)).astype(np.uint16)


def unstriped(offs):
    return offs[:16].T.reshape(-1).astype(np.int64)


E2M1 = np.array([0.0, 0.5, 1.0, 1.5, 2.0, 3.0, 4.0, 6.0, -0.0, -0.5, -1.0, -1.5, -2.0, -3.0, -4.0, -6.0])


def pack_weight(w, fmt):
    k, n = w.shape
    w = f64(np.asarray(w, np.float32).astype(ml_dtypes.bfloat16)).reshape(k // 32, 32, n)
    amax = np.abs(w).max(1)
    if fmt == "e4m3":
        byte = np.frexp(amax)[1] - 1 + 127 - 7
    else:
        mant, ex = np.frexp(amax / 6.0)
        byte = np.where(mant > 0.5, ex, ex - 1) + 127
    byte = np.clip(np.where(amax > 0, byte, 1), 1, 254)
    scaled = (w * np.exp2(127.0 - byte)[:, None, :]).reshape(k, n).astype(np.float32)
    by_word = np.ascontiguousarray(scaled.reshape(k // 512, 128, 4, n).transpose(0, 1, 3, 2))
    if fmt == "e4m3":
        words = by_word.astype(ml_dtypes.float8_e4m3fn).view(np.uint8)
    else:
        c = by_word.astype(ml_dtypes.float4_e2m1fn).view(np.uint8) & 0xF
        words = (c[..., 0::2] | (c[..., 1::2] << 4)).reshape(k // 512, 128, 2 * n)
    return np.ascontiguousarray(words), np.ascontiguousarray(byte.astype(np.uint8).reshape(k // 512, 16, n))


def unpack_weight(words, scales, fmt):
    g, _, n = scales.shape
    words = np.ascontiguousarray(words).reshape(g, 128, n, -1)
    if fmt == "e4m3":
        vals = words.view(ml_dtypes.float8_e4m3fn).astype(np.float64)
    else:
        nib = np.empty((g, 128, n, 4), np.uint8)
        nib[..., 0::2] = words & 0xF
        nib[..., 1::2] = words >> 4
        vals = E2M1[nib]
    vals = vals * np.repeat(np.exp2(scales.astype(np.float64) - 127.0), 8, axis=1)[..., None]
    return vals.transpose(0, 1, 3, 2).reshape(g * 512, n)


def gelu(v):
    return 0.5 * v * (1.0 + np.tanh(np.sqrt(2.0 / np.pi) * (v + 0.044715 * v**3)))


def bf(x):
    return np.asarray(x, np.float32).astype(ml_dtypes.bfloat16)


def planes(Y):
    n, m = Y.shape
    b = f64(bf(Y)).reshape(n // 32, 32, m)
    amax = np.abs(b).max(1)
    byte = np.clip(np.where(amax > 0, np.frexp(amax)[1] - 1 + 127 - 7, 1), 1, 254)
    codes = (b * np.exp2(127.0 - byte)[:, None, :]).reshape(n, m).astype(np.float32).astype(ml_dtypes.float8_e4m3fn).view(np.uint8)
    words = codes.reshape(n // 512, 128, 4, m).transpose(0, 1, 3, 2)
    return np.ascontiguousarray(words), np.ascontiguousarray(byte.astype(np.uint8).reshape(n // 512, 16, m))


K, T, S, H, T2, P, N = 1536, 4096, 1024, 512, 2048, 1024, 384


def setup_inputs():
    n = np.random.standard_normal
    s = mx_kscale(K)[:, None]
    u = mx_kscale(H)[:, None]
    d = {}
    d["tab_words"], d["tab_scales"] = pack_weight(n((K, T)) * s, "e4m3")
    d["offs"] = striped(np.random.permutation(T)[:S])
    d["w1"] = (n((K, H)) / s * u.T / K ** 0.5).astype(np.float32)
    d["ref"] = ((0.8 + 0.6 * n((H, S))) * u).astype(np.float32)
    d["page0"] = (n((H, T2)) * u).astype(np.float32)
    d["wgs"] = np.exp(0.3 * n((128, S))).astype(np.float32)
    d["offs2"] = striped(np.random.permutation(T2)[:S])
    d["offs3"] = striped(np.random.permutation(T2)[:P])
    d["bias"] = (0.6 * n(H) * u[:, 0]).astype(np.float32)
    d["w2_words"], d["w2_scales"] = pack_weight(n((H, H)) / u * u.T / H ** 0.5, "e2m1")
    d["w3"] = (n((H, N)) / u / H ** 0.5).astype(np.float32)
    return d


def reference(tab_words, tab_scales, offs, w1, ref, page0, wgs, offs2, offs3, bias, w2_words, w2_scales, w3):
    v = unpack_weight(tab_words, tab_scales, "e4m3")[:, unstriped(offs)]
    h = np.abs(mxq(f64(w1), 0, "e4m3").T @ v) - f64(ref)
    page = f64(page0).copy()
    page[:, unstriped(offs2)] = np.tile(f64(wgs), (H // 128, 1)) * h
    x = page[:, unstriped(offs3)] + f64(bias)[:, None]
    w2 = unpack_weight(w2_words, w2_scales, "e2m1")
    mix = w2.T @ mxq(x, 0, "e4m3")
    top = np.maximum(mix, x)
    y = mxq(f64(w3), 0, "e4m3").T @ mxq(top, 0, "e4m3")
    words, scales = planes(page)
    return y, page, words, scales

@@ -1,0 +1,287 @@
+from contextlib import ExitStack
+
+import concourse.mybir as mybir
+
+K, T, S, H, T2, PJ, N = 1536, 4096, 1024, 512, 2048, 1024, 384
+FLOPS = 2 * (K * H * S + H * H * PJ + H * N * PJ)
+
+F32 = mybir.dt.float32
+BF16 = mybir.dt.bfloat16
+U32 = mybir.dt.uint32
+I32 = mybir.dt.int32
+U16 = mybir.dt.uint16
+U8 = mybir.dt.uint8
+FP8X4 = mybir.dt.float8_e4m3fn_x4
+FP4X4 = mybir.dt.float4_e2m1fn_x4
+ALU = mybir.AluOpType
+ACT = mybir.ActivationFunctionType
+
+P = 128
+PACK = 4
+PASSES = K // (P * PACK)
+BANK = 512
+HALVES = S // BANK
+CHUNK = 256
+CHUNKS = PJ // CHUNK
+PIECE = 512
+PIECES = T2 // PIECE
+N_TILES = N // P
+
+
+def tile_list_pane_corrosion_page_kernel(
+    tc, tab_words, tab_scales, offs, w1, ref, page0, wgs, offs2, offs3, bias, w2_words, w2_scales, w3,
+    out_0, out_1, out_2, out_3,
+):
+    nc = tc.nc
+    with ExitStack() as ctx:
+        lists = ctx.enter_context(tc.tile_pool(name="lists", bufs=1))
+        keep = ctx.enter_context(tc.tile_pool(name="keep", bufs=1))
+        psum = ctx.enter_context(tc.psum_pool(name="psum", bufs=8))
+
+        idx1 = lists.tile([P, S // 16], U16, name="idx1")
+        idx2 = lists.tile([P, S // 16], U16, name="idx2")
+        idx3 = lists.tile([P, PJ // 16], U16, name="idx3")
+
+        def held(name, shape, dtype, tag=None, bufs=1):
+            return keep.tile(shape, dtype, name=name, tag=tag or name, bufs=bufs, align_bytes=64)
+
+        ref_rows = ref.rearrange("(p t) j -> p t j", t=PACK)
+        page_rows = page0.rearrange("(p t) j -> p t j", t=PACK)
+        out1_rows = out_1.rearrange("(p t) j -> p t j", t=PACK)
+        wgs_rows = wgs.rearrange("(s t) j -> s t j", t=PACK)
+
+        tab_sc = held("tab_sc", [P, T], U8)
+        w2_sc_raw = held("w2_sc_raw", [P, H], U8)
+        bias_col = held("bias_col", [P, PACK], F32)
+        nc.gpsimd.memset(tab_sc[:].bitcast(I32), 0)
+        nc.gpsimd.memset(w2_sc_raw[:].bitcast(I32), 0)
+        for q in range(4):
+            nc.gpsimd.dma_start(
+                out=tab_sc[32 * q : 32 * q + 4 * PASSES, :].bitcast(I32),
+                in_=tab_scales[:, 4 * q : 4 * q + 4, :].bitcast(I32),
+            )
+        nc.gpsimd.dma_start(out=bias_col[:], in_=bias.rearrange("(p t) -> p t", t=PACK))
+        for q in range(4):
+            nc.gpsimd.dma_start(
+                out=w2_sc_raw[32 * q : 32 * q + 4, :].bitcast(I32),
+                in_=w2_scales[0, 4 * q : 4 * q + 4, :].bitcast(I32),
+            )
+
+        w1_raw, tab = [], []
+        w2_raw = held("w2_raw", [P, 2 * H], U8)
+        for a in range(PASSES):
+            raw = held(f"w1_raw{a}", [P, PACK, H], F32, tag="raw", bufs=3)
+            nc.sync.dma_start(out=raw[:], in_=w1[a * 512 : (a + 1) * 512, :].rearrange("(p i) c -> p i c", i=PACK))
+            w1_raw.append(raw)
+            if a == 0:
+                nc.sync.dma_start(idx1[:], offs)
+            words = held(f"tab{a}", [P, T], U32)
+            nc.sync.dma_start(out=words[:].bitcast(I32), in_=tab_words[a].rearrange("p t i -> p (t i)").bitcast(I32))
+            tab.append(words)
+            if a == 0:
+                nc.sync.dma_start(out=w2_raw[:].bitcast(I32), in_=w2_words[0].bitcast(I32))
+                nc.sync.dma_start(idx2[:], offs2)
+                nc.sync.dma_start(idx3[:], offs3)
+
+        refs = [held(f"ref{t}", [P, S], F32, tag="ref", bufs=4) for t in range(PACK)]
+        pages = [held(f"page{t}", [P, T2], F32) for t in range(PACK)]
+        wgt = held("wgt", [P, PACK, S], F32, tag="wx")
+
+        def load_ref(t):
+            nc.sync.dma_start(out=refs[t][:], in_=ref_rows[:, t, :])
+
+        def load_page(t):
+            for q in range(4):
+                nc.sync.dma_start(out=wgt[32 * q : 32 * q + 32, t, :], in_=wgs_rows[:, t, :])
+            nc.sync.dma_start(out=pages[t][:], in_=page_rows[:, t, :])
+
+        load_ref(0)
+        load_page(0)
+        load_ref(1)
+        load_ref(2)
+        load_page(1)
+        load_ref(3)
+        load_page(2)
+        load_page(3)
+        w3_raw = held("w3_raw", [P, PACK, N], F32, tag="raw", bufs=3)
+        nc.sync.dma_start(out=w3_raw[:], in_=w3.rearrange("(p i) n -> p i n", i=PACK))
+
+        bias_wide = held("bias_wide", [P, PACK, CHUNK], F32)
+        nc.scalar.copy(out=bias_wide[:], in_=bias_col[:].unsqueeze(2).to_broadcast([P, PACK, CHUNK]))
+
+        w2_codes = held("w2_codes", [P, 2 * H], U8)
+        w2_sc = held("w2_sc", [P, H], U8)
+        got_sc = held("got_sc", [P, S], U8)
+        w1_codes = held("w1_codes", [P, PASSES, H], U32)
+        w1_sc = held("w1_sc", [P, PASSES, H], U8)
+        sums = [[psum.tile([P, BANK], F32, name=f"sum{t}_{u}", tag="bank") for u in range(HALVES)] for t in range(PACK)]
+        for a in range(PASSES):
+            grouped = held(f"w1_bf{a}", [P, H * PACK], BF16, tag="w_bf", bufs=2)
+            nc.scalar.copy(
+                out=grouped[:].rearrange("p (t m i) -> p m i t", t=PACK, i=PACK),
+                in_=w1_raw[a][:].rearrange("p i (m t) -> p m i t", t=PACK),
+            )
+            nc.vector.quantize_mx(out=w1_codes[:, a, :].bitcast(FP8X4), scales=w1_sc[:, a, :], in_=grouped[:])
+            got = held(f"got{a}", [P, S], U32)
+            if a == 0:
+                nc.vector.tensor_copy(out=got_sc[:], in_=tab_sc[:].indirect(idx1[:]))
+            for u in range(HALVES):
+                cols = slice(u * BANK, (u + 1) * BANK)
+                nc.vector.tensor_copy(out=got[:, cols], in_=tab[a][:].indirect(idx1[:, u * 32 : (u + 1) * 32]))
+            if a == 0:
+                nc.vector.tensor_copy(
+                    out=w2_codes[:].rearrange("p (t m b) -> p t m b", t=PACK, b=2),
+                    in_=w2_raw[:].rearrange("p (m t b) -> p t m b", t=PACK, b=2),
+                )
+                nc.vector.tensor_copy(
+                    out=w2_sc[:].rearrange("p (t m) -> p t m", t=PACK),
+                    in_=w2_sc_raw[:].rearrange("p (m t) -> p t m", t=PACK),
+                )
+            for t in range(PACK):
+                for u in range(HALVES):
+                    cols = slice(u * BANK, (u + 1) * BANK)
+                    rows = slice(t * P, (t + 1) * P)
+                    nc.tensor.matmul_mx(
+                        out=sums[t][u][:],
+                        lhsT=w1_codes[:, a, rows].bitcast(FP8X4),
+                        lhsT_scale=w1_sc[:, a, rows],
+                        rhs=got[:, cols].bitcast(FP8X4),
+                        rhs_scale=got_sc[4 * a : P, cols],
+                        start=(a == 0),
+                        stop=(a == PASSES - 1),
+                    )
+
+        page_bf = [held(f"page_bf{g}", [P, T2 // 2, PACK], BF16, tag="raw", bufs=3) for g in range(2)]
+        for t in range(PACK):
+            h = held(f"h{t}", [P, S], F32)
+            for u in range(HALVES):
+                cols = slice(u * BANK, (u + 1) * BANK)
+                nc.scalar.activation(out=h[:, cols], in_=sums[t][u][:], func=ACT.Abs)
+            steps = HALVES if t == 0 else 1
+            width = S // steps
+            for u in range(steps):
+                cols = slice(u * width, (u + 1) * width)
+                nc.vector.tensor_tensor(out=h[:, cols], in0=h[:, cols], in1=refs[t][:, cols], op=ALU.subtract)
+            for u in range(steps):
+                cols = slice(u * width, (u + 1) * width)
+                nc.vector.tensor_tensor(
+                    out=pages[t][:].indirect(idx2[:, u * width // 16 : (u + 1) * width // 16]),
+                    in0=h[:, cols], in1=wgt[:, t, cols], op=ALU.mult,
+                )
+            nc.sync.dma_start(out=out1_rows[:, t, :], in_=pages[t][:])
+            if t < PACK - 1:
+                for g in range(2):
+                    nc.scalar.copy(out=page_bf[g][:, :, t], in_=pages[t][:, g * (T2 // 2) : (g + 1) * (T2 // 2)])
+            if t == 1:
+                w3_bf = held("w3_bf", [P, N * PACK], BF16, tag="w_bf", bufs=2)
+                nc.scalar.copy(
+                    out=w3_bf[:].rearrange("p (n e i) -> p n i e", e=2, i=PACK),
+                    in_=w3_raw[:].rearrange("p i (n e) -> p n i e", e=2),
+                )
+        w3_codes = held("w3_codes", [P, N], U32)
+        w3_sc = held("w3_sc", [P, N], U8)
+        nc.vector.quantize_mx(out=w3_codes[:].bitcast(FP8X4), scales=w3_sc[:], in_=w3_bf[:])
+
+        x = held("x", [P, CHUNKS, PACK, CHUNK], F32, tag="wx")
+        for c in range(CHUNKS):
+            for t in range(PACK):
+                nc.vector.tensor_tensor(
+                    out=x[:, c, t, :], in0=pages[t][:].indirect(idx3[:, c * 16 : (c + 1) * 16]),
+                    in1=bias_wide[:, t, :], op=ALU.add,
+                )
+        x_bf = []
+        last = PACK - 1
+        for c in range(CHUNKS):
+            g, lo = divmod(c * PIECE, T2 // 2)
+            nc.scalar.copy(out=page_bf[g][:, lo : lo + PIECE, last], in_=pages[last][:, c * PIECE : (c + 1) * PIECE])
+            xb = held(f"x_bf{c}", [P, CHUNK * PACK], BF16)
+            nc.scalar.copy(
+                out=xb[:].rearrange("p (j e t) -> p j t e", e=2, t=PACK),
+                in_=x[:, c, :, :].rearrange("p t (j e) -> p j t e", e=2),
+            )
+            x_bf.append(xb)
+
+        x_codes = held("x_codes", [P, PJ], U32)
+        x_sc = held("x_sc", [P, PJ], U8)
+        top_codes = held("top_codes", [P, PJ], U32)
+        top_sc = held("top_sc", [P, PJ], U8)
+        page_codes = held("page_codes", [P, T2], U32)
+        page_sc = held("page_sc", [P, T2], U8)
+        out2_words = out_2[0].rearrange("p m t -> p (m t)").bitcast(I32)
+        out0_rows = out_0.rearrange("(n p) j -> p n j", p=P)
+        mixes, tops = {}, {}
+
+        def second_product(c):
+            cols = slice(c * CHUNK, (c + 1) * CHUNK)
+            nc.vector.quantize_mx(out=x_codes[:, cols].bitcast(FP8X4), scales=x_sc[:, cols], in_=x_bf[c][:])
+            for u in range(CHUNK // P):
+                mix = psum.tile([P, PACK, P], F32, name=f"mix{c}_{u}", tag="bank")
+                cu = slice(c * CHUNK + u * P, c * CHUNK + (u + 1) * P)
+                for t in range(PACK):
+                    nc.tensor.matmul_mx(
+                        out=mix[:, t, :],
+                        lhsT=w2_codes[:, 2 * P * t : 2 * P * (t + 1)].bitcast(FP4X4),
+                        lhsT_scale=w2_sc[:, P * t : P * (t + 1)],
+                        rhs=x_codes[:, cu].bitcast(FP8X4),
+                        rhs_scale=x_sc[:, cu],
+                        start=True,
+                        stop=True,
+                    )
+                mixes[c, u] = mix
+
+        def take_larger(c):
+            top = held(f"top{c}", [P, CHUNK * PACK], BF16, tag="top", bufs=2)
+            for u in range(CHUNK // P):
+                nc.vector.tensor_tensor(
+                    out=top[:, u * P * PACK : (u + 1) * P * PACK].rearrange("p (j e t) -> p j t e", e=2, t=PACK),
+                    in0=mixes[c, u][:].rearrange("p t (j e) -> p j t e", e=2),
+                    in1=x[:, c, :, u * P : (u + 1) * P].rearrange("p t (j e) -> p j t e", e=2),
+                    op=ALU.max,
+                )
+            tops[c] = top
+
+        def third_product(c):
+            cols = slice(c * CHUNK, (c + 1) * CHUNK)
+            nc.vector.quantize_mx(out=top_codes[:, cols].bitcast(FP8X4), scales=top_sc[:, cols], in_=tops[c][:])
+            y = held(f"y{c}", [P, N_TILES, CHUNK], F32, tag="ref", bufs=4)
+            for first, count in ((0, 2), (2, 1)):
+                acc = psum.tile([P, count, CHUNK], F32, name=f"acc{c}_{first}", tag="bank")
+                for n in range(count):
+                    rows = slice((first + n) * P, (first + n + 1) * P)
+                    nc.tensor.matmul_mx(
+                        out=acc[:, n, :],
+                        lhsT=w3_codes[:, rows].bitcast(FP8X4),
+                        lhsT_scale=w3_sc[:, rows],
+                        rhs=top_codes[:, cols].bitcast(FP8X4),
+                        rhs_scale=top_sc[:, cols],
+                        start=True,
+                        stop=True,
+                    )
+                nc.scalar.copy(out=y[:, first : first + count, :], in_=acc[:])
+            nc.sync.dma_start(out=out0_rows[:, :, cols], in_=y[:])
+
+        def page_planes(c):
+            g, lo = divmod(c * PIECE, T2 // 2)
+            cols = slice(c * PIECE, (c + 1) * PIECE)
+            nc.vector.quantize_mx(
+                out=page_codes[:, cols].bitcast(FP8X4),
+                scales=page_sc[:, cols],
+                in_=page_bf[g][:, lo : lo + PIECE, :].rearrange("p m t -> p (m t)"),
+            )
+            nc.sync.dma_start(out=out2_words[:, cols], in_=page_codes[:, cols].bitcast(I32))
+
+        second_product(0)
+        second_product(1)
+        page_planes(0)
+        for c in range(CHUNKS):
+            take_larger(c)
+            if c + 2 < CHUNKS:
+                second_product(c + 2)
+            if c >= CHUNKS - 2:
+                page_planes(c - 1)
+            third_product(c)
+        page_planes(PIECES - 1)
+        for q in range(4):
+            nc.sync.dma_start(
+                out=out_3[0, 4 * q : 4 * q + 4, :].bitcast(I32), in_=page_sc[32 * q : 32 * q + 4, :].bitcast(I32)
+            )

@@ -51,24 +51,36 @@ def tile_list_pane_corrosion_page_kernel(
         wgs_rows = wgs.rearrange("(s t) j -> s t j", t=PACK)
 
         tab_sc = held("tab_sc", [P, T], U8)
-        w2_sc_raw = held("w2_sc_raw", [P, H], U8)
-        bias_col = held("bias_col", [P, PACK], F32)
-        nc.gpsimd.memset(tab_sc[:].bitcast(I32), 0)
-        nc.gpsimd.memset(w2_sc_raw[:].bitcast(I32), 0)
+        nc.vector.memset(tab_sc[:].bitcast(I32), 0)
         for q in range(4):
-            nc.gpsimd.dma_start(
+            nc.scalar.dma_start(
                 out=tab_sc[32 * q : 32 * q + 4 * PASSES, :].bitcast(I32),
                 in_=tab_scales[:, 4 * q : 4 * q + 4, :].bitcast(I32),
             )
-        nc.gpsimd.dma_start(out=bias_col[:], in_=bias.rearrange("(p t) -> p t", t=PACK))
+
+        w2_raw = held("w2_raw", [P, 2 * H], U8)
+        w2_sc_raw = held("w2_sc_raw", [P, H], U8)
+        bias_col = held("bias_col", [P, PACK], F32)
+        w2_codes = held("w2_codes", [P, 2 * H], U8)
+        w2_sc = held("w2_sc", [P, H], U8)
+        nc.gpsimd.memset(w2_sc_raw[:].bitcast(I32), 0)
+        nc.gpsimd.dma_start(out=w2_raw[:].bitcast(I32), in_=w2_words[0].bitcast(I32))
         for q in range(4):
             nc.gpsimd.dma_start(
                 out=w2_sc_raw[32 * q : 32 * q + 4, :].bitcast(I32),
                 in_=w2_scales[0, 4 * q : 4 * q + 4, :].bitcast(I32),
             )
+        nc.gpsimd.dma_start(out=bias_col[:], in_=bias.rearrange("(p t) -> p t", t=PACK))
+        nc.gpsimd.tensor_copy(
+            out=w2_codes[:].rearrange("p (t m b) -> p t m b", t=PACK, b=2),
+            in_=w2_raw[:].rearrange("p (m t b) -> p t m b", t=PACK, b=2),
+        )
+        nc.gpsimd.tensor_copy(
+            out=w2_sc[:].rearrange("p (t m) -> p t m", t=PACK),
+            in_=w2_sc_raw[:].rearrange("p (m t) -> p t m", t=PACK),
+        )
 
         w1_raw, tab = [], []
-        w2_raw = held("w2_raw", [P, 2 * H], U8)
         for a in range(PASSES):
             raw = held(f"w1_raw{a}", [P, PACK, H], F32, tag="raw", bufs=3)
             nc.sync.dma_start(out=raw[:], in_=w1[a * 512 : (a + 1) * 512, :].rearrange("(p i) c -> p i c", i=PACK))
@@ -79,38 +91,27 @@ def tile_list_pane_corrosion_page_kernel(
             nc.sync.dma_start(out=words[:].bitcast(I32), in_=tab_words[a].rearrange("p t i -> p (t i)").bitcast(I32))
             tab.append(words)
             if a == 0:
-                nc.sync.dma_start(out=w2_raw[:].bitcast(I32), in_=w2_words[0].bitcast(I32))
                 nc.sync.dma_start(idx2[:], offs2)
                 nc.sync.dma_start(idx3[:], offs3)
 
         refs = [held(f"ref{t}", [P, S], F32, tag="ref", bufs=4) for t in range(PACK)]
         pages = [held(f"page{t}", [P, T2], F32) for t in range(PACK)]
-        wgt = held("wgt", [P, PACK, S], F32, tag="wx")
+        wgt = held("wgt", [P, PACK, S], F32)
 
-        def load_ref(t):
-            nc.sync.dma_start(out=refs[t][:], in_=ref_rows[:, t, :])
+        def load_factors(t, cols):
+            nc.sync.dma_start(out=refs[t][:, cols], in_=ref_rows[:, t, cols])
+            for q in (0, 2, 1, 3):
+                nc.sync.dma_start(out=wgt[32 * q : 32 * q + 32, t, cols], in_=wgs_rows[:, t, cols])
 
-        def load_page(t):
-            for q in range(4):
-                nc.sync.dma_start(out=wgt[32 * q : 32 * q + 32, t, :], in_=wgs_rows[:, t, :])
+        load_factors(0, slice(0, BANK))
+        nc.sync.dma_start(out=pages[0][:], in_=page_rows[:, 0, :])
+        load_factors(0, slice(BANK, S))
+        for t in range(1, PACK):
+            load_factors(t, slice(0, S))
             nc.sync.dma_start(out=pages[t][:], in_=page_rows[:, t, :])
-
-        load_ref(0)
-        load_page(0)
-        load_ref(1)
-        load_ref(2)
-        load_page(1)
-        load_ref(3)
-        load_page(2)
-        load_page(3)
         w3_raw = held("w3_raw", [P, PACK, N], F32, tag="raw", bufs=3)
         nc.sync.dma_start(out=w3_raw[:], in_=w3.rearrange("(p i) n -> p i n", i=PACK))
 
-        bias_wide = held("bias_wide", [P, PACK, CHUNK], F32)
-        nc.scalar.copy(out=bias_wide[:], in_=bias_col[:].unsqueeze(2).to_broadcast([P, PACK, CHUNK]))
-
-        w2_codes = held("w2_codes", [P, 2 * H], U8)
-        w2_sc = held("w2_sc", [P, H], U8)
         got_sc = held("got_sc", [P, S], U8)
         w1_codes = held("w1_codes", [P, PASSES, H], U32)
         w1_sc = held("w1_sc", [P, PASSES, H], U8)
@@ -128,15 +129,6 @@ def tile_list_pane_corrosion_page_kernel(
             for u in range(HALVES):
                 cols = slice(u * BANK, (u + 1) * BANK)
                 nc.vector.tensor_copy(out=got[:, cols], in_=tab[a][:].indirect(idx1[:, u * 32 : (u + 1) * 32]))
-            if a == 0:
-                nc.vector.tensor_copy(
-                    out=w2_codes[:].rearrange("p (t m b) -> p t m b", t=PACK, b=2),
-                    in_=w2_raw[:].rearrange("p (m t b) -> p t m b", t=PACK, b=2),
-                )
-                nc.vector.tensor_copy(
-                    out=w2_sc[:].rearrange("p (t m) -> p t m", t=PACK),
-                    in_=w2_sc_raw[:].rearrange("p (m t) -> p t m", t=PACK),
-                )
             for t in range(PACK):
                 for u in range(HALVES):
                     cols = slice(u * BANK, (u + 1) * BANK)
@@ -152,21 +144,23 @@ def tile_list_pane_corrosion_page_kernel(
                     )
 
         page_bf = [held(f"page_bf{g}", [P, T2 // 2, PACK], BF16, tag="raw", bufs=3) for g in range(2)]
+        h_all = held("h_all", [P, PACK, S], F32, tag="hx")
         for t in range(PACK):
-            h = held(f"h{t}", [P, S], F32)
+            h = h_all[:, t, :]
             for u in range(HALVES):
                 cols = slice(u * BANK, (u + 1) * BANK)
                 nc.scalar.activation(out=h[:, cols], in_=sums[t][u][:], func=ACT.Abs)
+            for u in range(HALVES):
+                cols = slice(u * BANK, (u + 1) * BANK)
+                engine = nc.vector if (t, u) == (0, 0) else nc.gpsimd
+                engine.tensor_tensor(out=h[:, cols], in0=h[:, cols], in1=refs[t][:, cols], op=ALU.subtract)
+                engine.tensor_tensor(out=h[:, cols], in0=h[:, cols], in1=wgt[:, t, cols], op=ALU.mult)
             steps = HALVES if t == 0 else 1
             width = S // steps
             for u in range(steps):
                 cols = slice(u * width, (u + 1) * width)
-                nc.vector.tensor_tensor(out=h[:, cols], in0=h[:, cols], in1=refs[t][:, cols], op=ALU.subtract)
-            for u in range(steps):
-                cols = slice(u * width, (u + 1) * width)
-                nc.vector.tensor_tensor(
-                    out=pages[t][:].indirect(idx2[:, u * width // 16 : (u + 1) * width // 16]),
-                    in0=h[:, cols], in1=wgt[:, t, cols], op=ALU.mult,
+                nc.vector.tensor_copy(
+                    out=pages[t][:].indirect(idx2[:, u * width // 16 : (u + 1) * width // 16]), in_=h[:, cols]
                 )
             nc.sync.dma_start(out=out1_rows[:, t, :], in_=pages[t][:])
             if t < PACK - 1:
@@ -182,12 +176,13 @@ def tile_list_pane_corrosion_page_kernel(
         w3_sc = held("w3_sc", [P, N], U8)
         nc.vector.quantize_mx(out=w3_codes[:].bitcast(FP8X4), scales=w3_sc[:], in_=w3_bf[:])
 
-        x = held("x", [P, CHUNKS, PACK, CHUNK], F32, tag="wx")
+        x = held("x", [P, CHUNKS, PACK, CHUNK], F32, tag="hx")
         for c in range(CHUNKS):
             for t in range(PACK):
-                nc.vector.tensor_tensor(
-                    out=x[:, c, t, :], in0=pages[t][:].indirect(idx3[:, c * 16 : (c + 1) * 16]),
-                    in1=bias_wide[:, t, :], op=ALU.add,
+                nc.vector.tensor_copy(out=x[:, c, t, :], in_=pages[t][:].indirect(idx3[:, c * 16 : (c + 1) * 16]))
+                nc.gpsimd.tensor_scalar(
+                    out=x[:, c, t, :], in0=x[:, c, t, :], scalar1=bias_col[:, t : t + 1], scalar2=1.0,
+                    op0=ALU.add, op1=ALU.mult,
                 )
         x_bf = []
         last = PACK - 1

from contextlib import ExitStack

import concourse.mybir as mybir

K, T, S, H, T2, PJ, N = 1536, 4096, 1024, 512, 2048, 1024, 384
FLOPS = 2 * (K * H * S + H * H * PJ + H * N * PJ)

F32 = mybir.dt.float32
BF16 = mybir.dt.bfloat16
U32 = mybir.dt.uint32
I32 = mybir.dt.int32
U16 = mybir.dt.uint16
U8 = mybir.dt.uint8
FP8X4 = mybir.dt.float8_e4m3fn_x4
FP4X4 = mybir.dt.float4_e2m1fn_x4
ALU = mybir.AluOpType
ACT = mybir.ActivationFunctionType

P = 128
PACK = 4
PASSES = K // (P * PACK)
BANK = 512
HALVES = S // BANK
CHUNK = 256
CHUNKS = PJ // CHUNK
PIECE = 512
PIECES = T2 // PIECE
N_TILES = N // P


def tile_list_pane_corrosion_page_kernel(
    tc, tab_words, tab_scales, offs, w1, ref, page0, wgs, offs2, offs3, bias, w2_words, w2_scales, w3,
    out_0, out_1, out_2, out_3,
):
    nc = tc.nc
    with ExitStack() as ctx:
        lists = ctx.enter_context(tc.tile_pool(name="lists", bufs=1))
        keep = ctx.enter_context(tc.tile_pool(name="keep", bufs=1))
        psum = ctx.enter_context(tc.psum_pool(name="psum", bufs=8))

        idx1 = lists.tile([P, S // 16], U16, name="idx1")
        idx2 = lists.tile([P, S // 16], U16, name="idx2")
        idx3 = lists.tile([P, PJ // 16], U16, name="idx3")

        def held(name, shape, dtype, tag=None, bufs=1):
            return keep.tile(shape, dtype, name=name, tag=tag or name, bufs=bufs, align_bytes=64)

        ref_rows = ref.rearrange("(p t) j -> p t j", t=PACK)
        page_rows = page0.rearrange("(p t) j -> p t j", t=PACK)
        out1_rows = out_1.rearrange("(p t) j -> p t j", t=PACK)
        wgs_rows = wgs.rearrange("(s t) j -> s t j", t=PACK)

        tab_sc = held("tab_sc", [P, T], U8)
        nc.vector.memset(tab_sc[:].bitcast(I32), 0)
        for q in range(4):
            nc.scalar.dma_start(
                out=tab_sc[32 * q : 32 * q + 4 * PASSES, :].bitcast(I32),
                in_=tab_scales[:, 4 * q : 4 * q + 4, :].bitcast(I32),
            )

        w2_raw = held("w2_raw", [P, 2 * H], U8)
        w2_sc_raw = held("w2_sc_raw", [P, H], U8)
        bias_col = held("bias_col", [P, PACK], F32)
        w2_codes = held("w2_codes", [P, 2 * H], U8)
        w2_sc = held("w2_sc", [P, H], U8)
        nc.gpsimd.memset(w2_sc_raw[:].bitcast(I32), 0)
        nc.gpsimd.dma_start(out=w2_raw[:].bitcast(I32), in_=w2_words[0].bitcast(I32))
        for q in range(4):
            nc.gpsimd.dma_start(
                out=w2_sc_raw[32 * q : 32 * q + 4, :].bitcast(I32),
                in_=w2_scales[0, 4 * q : 4 * q + 4, :].bitcast(I32),
            )
        nc.gpsimd.dma_start(out=bias_col[:], in_=bias.rearrange("(p t) -> p t", t=PACK))
        nc.gpsimd.tensor_copy(
            out=w2_codes[:].rearrange("p (t m b) -> p t m b", t=PACK, b=2),
            in_=w2_raw[:].rearrange("p (m t b) -> p t m b", t=PACK, b=2),
        )
        nc.gpsimd.tensor_copy(
            out=w2_sc[:].rearrange("p (t m) -> p t m", t=PACK),
            in_=w2_sc_raw[:].rearrange("p (m t) -> p t m", t=PACK),
        )

        w1_raw, tab = [], []
        for a in range(PASSES):
            raw = held(f"w1_raw{a}", [P, PACK, H], F32, tag="raw", bufs=3)
            nc.sync.dma_start(out=raw[:], in_=w1[a * 512 : (a + 1) * 512, :].rearrange("(p i) c -> p i c", i=PACK))
            w1_raw.append(raw)
            if a == 0:
                nc.sync.dma_start(idx1[:], offs)
            words = held(f"tab{a}", [P, T], U32)
            nc.sync.dma_start(out=words[:].bitcast(I32), in_=tab_words[a].rearrange("p t i -> p (t i)").bitcast(I32))
            tab.append(words)
            if a == 0:
                nc.sync.dma_start(idx2[:], offs2)
                nc.sync.dma_start(idx3[:], offs3)

        refs = [held(f"ref{t}", [P, S], F32, tag="ref", bufs=4) for t in range(PACK)]
        pages = [held(f"page{t}", [P, T2], F32) for t in range(PACK)]
        wgt = held("wgt", [P, PACK, S], F32)

        def load_factors(t, cols):
            nc.sync.dma_start(out=refs[t][:, cols], in_=ref_rows[:, t, cols])
            for q in (0, 2, 1, 3):
                nc.sync.dma_start(out=wgt[32 * q : 32 * q + 32, t, cols], in_=wgs_rows[:, t, cols])

        load_factors(0, slice(0, BANK))
        nc.sync.dma_start(out=pages[0][:], in_=page_rows[:, 0, :])
        load_factors(0, slice(BANK, S))
        for t in range(1, PACK):
            load_factors(t, slice(0, S))
            nc.sync.dma_start(out=pages[t][:], in_=page_rows[:, t, :])
        w3_raw = held("w3_raw", [P, PACK, N], F32, tag="raw", bufs=3)
        nc.sync.dma_start(out=w3_raw[:], in_=w3.rearrange("(p i) n -> p i n", i=PACK))

        got_sc = held("got_sc", [P, S], U8)
        w1_codes = held("w1_codes", [P, PASSES, H], U32)
        w1_sc = held("w1_sc", [P, PASSES, H], U8)
        sums = [[psum.tile([P, BANK], F32, name=f"sum{t}_{u}", tag="bank") for u in range(HALVES)] for t in range(PACK)]
        for a in range(PASSES):
            grouped = held(f"w1_bf{a}", [P, H * PACK], BF16, tag="w_bf", bufs=2)
            nc.scalar.copy(
                out=grouped[:].rearrange("p (t m i) -> p m i t", t=PACK, i=PACK),
                in_=w1_raw[a][:].rearrange("p i (m t) -> p m i t", t=PACK),
            )
            nc.vector.quantize_mx(out=w1_codes[:, a, :].bitcast(FP8X4), scales=w1_sc[:, a, :], in_=grouped[:])
            got = held(f"got{a}", [P, S], U32)
            if a == 0:
                nc.vector.tensor_copy(out=got_sc[:], in_=tab_sc[:].indirect(idx1[:]))
            for u in range(HALVES):
                cols = slice(u * BANK, (u + 1) * BANK)
                nc.vector.tensor_copy(out=got[:, cols], in_=tab[a][:].indirect(idx1[:, u * 32 : (u + 1) * 32]))
            for t in range(PACK):
                for u in range(HALVES):
                    cols = slice(u * BANK, (u + 1) * BANK)
                    rows = slice(t * P, (t + 1) * P)
                    nc.tensor.matmul_mx(
                        out=sums[t][u][:],
                        lhsT=w1_codes[:, a, rows].bitcast(FP8X4),
                        lhsT_scale=w1_sc[:, a, rows],
                        rhs=got[:, cols].bitcast(FP8X4),
                        rhs_scale=got_sc[4 * a : P, cols],
                        start=(a == 0),
                        stop=(a == PASSES - 1),
                    )

        page_bf = [held(f"page_bf{g}", [P, T2 // 2, PACK], BF16, tag="raw", bufs=3) for g in range(2)]
        h_all = held("h_all", [P, PACK, S], F32, tag="hx")
        for t in range(PACK):
            h = h_all[:, t, :]
            for u in range(HALVES):
                cols = slice(u * BANK, (u + 1) * BANK)
                nc.scalar.activation(out=h[:, cols], in_=sums[t][u][:], func=ACT.Abs)
            for u in range(HALVES):
                cols = slice(u * BANK, (u + 1) * BANK)
                engine = nc.vector if (t, u) == (0, 0) else nc.gpsimd
                engine.tensor_tensor(out=h[:, cols], in0=h[:, cols], in1=refs[t][:, cols], op=ALU.subtract)
                engine.tensor_tensor(out=h[:, cols], in0=h[:, cols], in1=wgt[:, t, cols], op=ALU.mult)
            steps = HALVES if t == 0 else 1
            width = S // steps
            for u in range(steps):
                cols = slice(u * width, (u + 1) * width)
                nc.vector.tensor_copy(
                    out=pages[t][:].indirect(idx2[:, u * width // 16 : (u + 1) * width // 16]), in_=h[:, cols]
                )
            nc.sync.dma_start(out=out1_rows[:, t, :], in_=pages[t][:])
            if t < PACK - 1:
                for g in range(2):
                    nc.scalar.copy(out=page_bf[g][:, :, t], in_=pages[t][:, g * (T2 // 2) : (g + 1) * (T2 // 2)])
            if t == 1:
                w3_bf = held("w3_bf", [P, N * PACK], BF16, tag="w_bf", bufs=2)
                nc.scalar.copy(
                    out=w3_bf[:].rearrange("p (n e i) -> p n i e", e=2, i=PACK),
                    in_=w3_raw[:].rearrange("p i (n e) -> p n i e", e=2),
                )
        w3_codes = held("w3_codes", [P, N], U32)
        w3_sc = held("w3_sc", [P, N], U8)
        nc.vector.quantize_mx(out=w3_codes[:].bitcast(FP8X4), scales=w3_sc[:], in_=w3_bf[:])

        x = held("x", [P, CHUNKS, PACK, CHUNK], F32, tag="hx")
        for c in range(CHUNKS):
            for t in range(PACK):
                nc.vector.tensor_copy(out=x[:, c, t, :], in_=pages[t][:].indirect(idx3[:, c * 16 : (c + 1) * 16]))
                nc.gpsimd.tensor_scalar(
                    out=x[:, c, t, :], in0=x[:, c, t, :], scalar1=bias_col[:, t : t + 1], scalar2=1.0,
                    op0=ALU.add, op1=ALU.mult,
                )
        x_bf = []
        last = PACK - 1
        for c in range(CHUNKS):
            g, lo = divmod(c * PIECE, T2 // 2)
            nc.scalar.copy(out=page_bf[g][:, lo : lo + PIECE, last], in_=pages[last][:, c * PIECE : (c + 1) * PIECE])
            xb = held(f"x_bf{c}", [P, CHUNK * PACK], BF16)
            nc.scalar.copy(
                out=xb[:].rearrange("p (j e t) -> p j t e", e=2, t=PACK),
                in_=x[:, c, :, :].rearrange("p t (j e) -> p j t e", e=2),
            )
            x_bf.append(xb)

        x_codes = held("x_codes", [P, PJ], U32)
        x_sc = held("x_sc", [P, PJ], U8)
        top_codes = held("top_codes", [P, PJ], U32)
        top_sc = held("top_sc", [P, PJ], U8)
        page_codes = held("page_codes", [P, T2], U32)
        page_sc = held("page_sc", [P, T2], U8)
        out2_words = out_2[0].rearrange("p m t -> p (m t)").bitcast(I32)
        out0_rows = out_0.rearrange("(n p) j -> p n j", p=P)
        mixes, tops = {}, {}

        def second_product(c):
            cols = slice(c * CHUNK, (c + 1) * CHUNK)
            nc.vector.quantize_mx(out=x_codes[:, cols].bitcast(FP8X4), scales=x_sc[:, cols], in_=x_bf[c][:])
            for u in range(CHUNK // P):
                mix = psum.tile([P, PACK, P], F32, name=f"mix{c}_{u}", tag="bank")
                cu = slice(c * CHUNK + u * P, c * CHUNK + (u + 1) * P)
                for t in range(PACK):
                    nc.tensor.matmul_mx(
                        out=mix[:, t, :],
                        lhsT=w2_codes[:, 2 * P * t : 2 * P * (t + 1)].bitcast(FP4X4),
                        lhsT_scale=w2_sc[:, P * t : P * (t + 1)],
                        rhs=x_codes[:, cu].bitcast(FP8X4),
                        rhs_scale=x_sc[:, cu],
                        start=True,
                        stop=True,
                    )
                mixes[c, u] = mix

        def take_larger(c):
            top = held(f"top{c}", [P, CHUNK * PACK], BF16, tag="top", bufs=2)
            for u in range(CHUNK // P):
                nc.vector.tensor_tensor(
                    out=top[:, u * P * PACK : (u + 1) * P * PACK].rearrange("p (j e t) -> p j t e", e=2, t=PACK),
                    in0=mixes[c, u][:].rearrange("p t (j e) -> p j t e", e=2),
                    in1=x[:, c, :, u * P : (u + 1) * P].rearrange("p t (j e) -> p j t e", e=2),
                    op=ALU.max,
                )
            tops[c] = top

        def third_product(c):
            cols = slice(c * CHUNK, (c + 1) * CHUNK)
            nc.vector.quantize_mx(out=top_codes[:, cols].bitcast(FP8X4), scales=top_sc[:, cols], in_=tops[c][:])
            y = held(f"y{c}", [P, N_TILES, CHUNK], F32, tag="ref", bufs=4)
            for first, count in ((0, 2), (2, 1)):
                acc = psum.tile([P, count, CHUNK], F32, name=f"acc{c}_{first}", tag="bank")
                for n in range(count):
                    rows = slice((first + n) * P, (first + n + 1) * P)
                    nc.tensor.matmul_mx(
                        out=acc[:, n, :],
                        lhsT=w3_codes[:, rows].bitcast(FP8X4),
                        lhsT_scale=w3_sc[:, rows],
                        rhs=top_codes[:, cols].bitcast(FP8X4),
                        rhs_scale=top_sc[:, cols],
                        start=True,
                        stop=True,
                    )
                nc.scalar.copy(out=y[:, first : first + count, :], in_=acc[:])
            nc.sync.dma_start(out=out0_rows[:, :, cols], in_=y[:])

        def page_planes(c):
            g, lo = divmod(c * PIECE, T2 // 2)
            cols = slice(c * PIECE, (c + 1) * PIECE)
            nc.vector.quantize_mx(
                out=page_codes[:, cols].bitcast(FP8X4),
                scales=page_sc[:, cols],
                in_=page_bf[g][:, lo : lo + PIECE, :].rearrange("p m t -> p (m t)"),
            )
            nc.sync.dma_start(out=out2_words[:, cols], in_=page_codes[:, cols].bitcast(I32))

        second_product(0)
        second_product(1)
        page_planes(0)
        for c in range(CHUNKS):
            take_larger(c)
            if c + 2 < CHUNKS:
                second_product(c + 2)
            if c >= CHUNKS - 2:
                page_planes(c - 1)
            third_product(c)
        page_planes(PIECES - 1)
        for q in range(4):
            nc.sync.dma_start(
                out=out_3[0, 4 * q : 4 * q + 4, :].bitcast(I32), in_=page_sc[32 * q : 32 * q + 4, :].bitcast(I32)
            )
